import numpy as np
import ml_dtypes


def mxq(x, axis, fmt="e4m3"):
    dtype, down = {"e4m3": (ml_dtypes.float8_e4m3fn, 7), "e5m2": (ml_dtypes.float8_e5m2, 14)}[fmt]
    v = np.moveaxis(np.asarray(x, np.float32).astype(ml_dtypes.bfloat16).astype(np.float64), axis, -1)
    blocks = v.reshape(v.shape[:-1] + (-1, 32))
    amax = np.abs(blocks).max(-1, keepdims=True)
    byte = np.maximum(np.where(amax > 0, np.frexp(amax)[1] - 1 + 127, 0) - down, 1)
    scale = np.exp2(byte - 127.0)
    codes = (blocks / scale).astype(np.float32).astype(dtype).astype(np.float64)
    return np.moveaxis((codes * scale).reshape(v.shape), -1, axis)


WIDE = False


def mx_kscale(k):
    if not WIDE:
        return np.ones(k)
    levels = np.array([10, -10, 5, -5, 0])
    if k % 512:
        return np.exp2(np.random.permutation(np.resize(levels, k // 32))).repeat(32)
    a = np.empty((k // 512, 16))
    for p in range(k // 512):
        a[p, :8] = np.random.permutation(np.resize(levels, 8))
        for g in range(8):
            far = levels[np.abs(levels - a[p, g]) >= 10]
            a[p, g + 8] = far[np.random.randint(len(far))]
    return np.exp2(a.ravel()).repeat(32)


def f64(x):
    return np.asarray(x).astype(np.float64)


def striped(idx):
    return np.tile(idx.reshape(-1, 16).T, (8, 1)).astype(np.uint16)


def unstriped(offs):
    return offs[:16].T.reshape(-1).astype(np.int64)


def striped8(idx):
    return np.concatenate([x.reshape(-1, 16).T for x in idx]).astype(np.uint16)


def runs(offs, k):
    lists = np.stack([offs[16 * r : 16 * r + 16].T.reshape(-1) for r in range(8)]).astype(np.int64)
    return lists[np.arange(k) % 512 // 64]


def pack_weight(w):
    k, n = w.shape
    w = f64(np.asarray(w, np.float32).astype(ml_dtypes.bfloat16)).reshape(k // 32, 32, n)
    amax = np.abs(w).max(1)
    byte = np.clip(np.where(amax > 0, np.frexp(amax)[1] - 1 + 127 - 7, 1), 1, 254)
    scaled = (w * np.exp2(127.0 - byte)[:, None, :]).reshape(k, n).astype(np.float32)
    words = np.ascontiguousarray(scaled.reshape(k // 512, 128, 4, n).transpose(0, 1, 3, 2)).astype(ml_dtypes.float8_e4m3fn).view(np.uint8)
    return words, np.ascontiguousarray(byte.astype(np.uint8).reshape(k // 512, 16, n))


def unpack_weight(words, scales):
    g, p, n, _ = words.shape
    vals = np.ascontiguousarray(words).view(ml_dtypes.float8_e4m3fn).astype(np.float64) * np.repeat(np.exp2(scales.astype(np.float64) - 127.0), 8, axis=1)[..., None]
    return vals.transpose(0, 1, 3, 2).reshape(g * 512, n)


K, T, S, H, W = 512, 2048, 512, 512, 256


def setup_inputs():
    n = np.random.standard_normal
    s = mx_kscale(K)[:, None]
    u = mx_kscale(S)
    packed_xT = pack_weight(n((K, T)) * s)
    return {
        "x_words": packed_xT[0],
        "x_scales": packed_xT[1],
        "wa": (n((K, H)) / np.sqrt(K) / s).astype(np.float32),
        "wb": (n((K, H)) / np.sqrt(K) / s).astype(np.float32),
        "gt": (np.random.uniform(0.5, 1.5, (S, 1)) * u[:, None]).astype(np.float32),
        "gi": (np.random.uniform(0.5, 1.5, (S, 1)) / u[:, None]).astype(np.float32),
        "offs": striped(np.random.permutation(T)[:S]),
        "two": striped(np.random.permutation(T)[:S]),
        "n1": striped(np.random.permutation(H)[:W]),
        "n2": striped(np.random.permutation(H)[:W]),
        "n3": striped8(np.stack([np.random.permutation(H) for _ in range(8)])),
        "n4": striped8(np.stack([np.random.permutation(H) for _ in range(8)])),
    }


def reference(x_words, x_scales, wa, wb, gt, gi, offs, two, n1, n2, n3, n4):
    x_two = unpack_weight(x_words, x_scales)[:, unstriped(two)]
    b = x_two.T @ mxq(f64(wb), 0, "e4m3")
    xq = unpack_weight(x_words, x_scales)[:, unstriped(offs)]
    a = xq.T @ mxq(f64(wa), 0, "e4m3")
    ra = b[:, unstriped(n2)] - (0.5 * a[:, unstriped(n1)])
    ds = a.copy()
    ds[:, unstriped(n1)] = ra
    z = f64(gt) * ds
    z2 = f64(gi) * b
    cv = 0.0625 * ((mxq(z, 0, "e4m3").T @ mxq(z2, 0, "e4m3")))
    return (cv[np.arange(H)[:, None], runs(n3, H)]) / (np.abs(cv) + np.abs(cv[np.arange(H)[:, None], runs(n4, H)]) + 0.5)

@@ -1,0 +1,258 @@
+from contextlib import ExitStack
+
+import concourse.mybir as mybir
+from concourse.masks import make_identity
+
+F32 = mybir.dt.float32
+BF16 = mybir.dt.bfloat16
+I32 = mybir.dt.int32
+U32 = mybir.dt.uint32
+U16 = mybir.dt.uint16
+U8 = mybir.dt.uint8
+FP8X4 = mybir.dt.float8_e4m3fn_x4
+ALU = mybir.AluOpType
+ACT = mybir.ActivationFunctionType
+
+K, T, S, H, W = 512, 2048, 512, 512, 256
+P = 128
+PACK = 4
+HALF = H // 2
+FLOPS = 2 * (2 * K * S * H + S * H * H)
+
+
+def tile_picked_momtputbnorm2_none_p_kernel(tc, x_words, x_scales, wa, wb, gt, gi, offs, two, n1, n2, n3, n4, out):
+    nc = tc.nc
+    with ExitStack() as ctx:
+        lists = ctx.enter_context(tc.tile_pool(name="lists", bufs=1))
+        sb = ctx.enter_context(tc.tile_pool(name="sb", bufs=1))
+        psum = ctx.enter_context(tc.psum_pool(name="psum", bufs=1))
+
+        def load_list(src, name):
+            tile = lists.tile(list(src.shape), U16, name=name)
+            nc.sync.dma_start(tile[:], src)
+            return tile
+
+        def tile(shape, dtype, name):
+            return sb.tile(shape, dtype, name=name, align_bytes=64)
+
+        banks = [psum.tile([P, H], F32, name=f"bank{i}") for i in range(8)]
+
+        table_scales = tile([P, T], U8, "table_scales")
+        nc.gpsimd.memset(table_scales[:].bitcast(I32), 0)
+        for quad in range(4):
+            nc.sync.dma_start(table_scales[32 * quad : 32 * quad + 4, :].bitcast(I32), x_scales[0, 4 * quad : 4 * quad + 4, :].bitcast(I32))
+        two_l = load_list(two, "two_l")
+        offs_l = load_list(offs, "offs_l")
+        table_words = tile([P, T], U32, "table_words")
+        nc.sync.dma_start(table_words[:].bitcast(I32), x_words[0].rearrange("p n j -> p (n j)").bitcast(I32))
+        halves = [slice(0, HALF), slice(HALF, H)]
+
+        def load_weights(w, name):
+            raws = [tile([P, PACK, HALF], F32, f"{name}{h}") for h in range(2)]
+            for h in range(2):
+                nc.sync.dma_start(raws[h][:], w.rearrange("(p j) c -> p j c", j=PACK)[:, :, halves[h]])
+            return raws
+
+        wb_raw = load_weights(wb, "wb_raw")
+        wa_raw = load_weights(wa, "wa_raw")
+        n2_l = load_list(n2, "n2_l")
+        n1_l = load_list(n1, "n1_l")
+        n4_l = load_list(n4, "n4_l")
+        n3_l = load_list(n3, "n3_l")
+        gain_rows = tile([P, P], F32, "gain_rows")
+        nc.gpsimd.memset(gain_rows[:], 0.0)
+        for first, src in ((0, gt), (PACK, gi)):
+            nc.gpsimd.dma_start(
+                gain_rows[first : first + PACK, :].rearrange("t (q r) -> t q r", r=8),
+                src.rearrange("(q t r) o -> t q (r o)", t=PACK, r=8),
+            )
+        identity = tile([P, P], F32, "identity")
+        make_identity(nc, identity[:])
+
+        def pick_scales(lst, name):
+            picked = tile([P, S], U8, name + "_picked")
+            nc.vector.tensor_copy(picked[:], table_scales[:].indirect(lst[:]))
+            dealt = tile([P, S], U8, name + "_dealt")
+            nc.vector.tensor_copy(
+                dealt[:].bitcast(I32).rearrange("p (t q w) -> p t q w", t=PACK, w=2),
+                picked[:].bitcast(I32).rearrange("p (q t w) -> p t q w", t=PACK, w=2),
+            )
+            return dealt
+
+        def pick_words(lst, name):
+            picked = tile([P, S], U32, name)
+            nc.vector.tensor_copy(picked[:].rearrange("p (t q r) -> p q t r", t=PACK, r=8), table_words[:].indirect(lst[:]))
+            return picked
+
+        def round_weights(raw, name):
+            grouped = tile([P, HALF * PACK], BF16, name)
+            nc.scalar.copy(
+                grouped[:].rearrange("p (c i j) -> p c j i", i=4, j=PACK),
+                raw[:].rearrange("p j (c i) -> p c j i", i=4),
+            )
+            return grouped
+
+        def quantize(codes, scales, cols, values):
+            nc.vector.quantize_mx(out=codes[:, cols].bitcast(FP8X4), scales=scales[:, cols], in_=values)
+
+        def product(bank, l_codes, l_scales, block, r_codes, r_scales):
+            cols = slice(block * P, (block + 1) * P)
+            nc.tensor.matmul_mx(
+                out=bank[:], lhsT=l_codes[:, cols].bitcast(FP8X4), lhsT_scale=l_scales[:, cols],
+                rhs=r_codes[:].bitcast(FP8X4), rhs_scale=r_scales[:], start=True, stop=True,
+            )
+
+        two_scales = pick_scales(two_l, "two_scales")
+        offs_scales = pick_scales(offs_l, "offs_scales")
+        two_words = pick_words(two_l, "two_words")
+        offs_words = pick_words(offs_l, "offs_words")
+
+        wb_codes, wb_scales = tile([P, H], U32, "wb_codes"), tile([P, H], U8, "wb_scales")
+        wa_codes, wa_scales = tile([P, H], U32, "wa_codes"), tile([P, H], U8, "wa_scales")
+        for h in range(2):
+            quantize(wb_codes, wb_scales, halves[h], round_weights(wb_raw[h], f"wb_grouped{h}")[:])
+        for t in range(PACK):
+            product(banks[t], two_words, two_scales, t, wb_codes, wb_scales)
+        for h in range(2):
+            quantize(wa_codes, wa_scales, halves[h], round_weights(wa_raw[h], f"wa_grouped{h}")[:])
+        for t in range(PACK):
+            product(banks[PACK + t], offs_words, offs_scales, t, wa_codes, wa_scales)
+
+        b_rows, b_picked = [], []
+        for t in range(PACK):
+            rows = tile([P, H], F32, f"b_rows{t}")
+            nc.vector.tensor_copy(rows[:], banks[t][:])
+            picked = tile([P, W], F32, f"b_picked{t}")
+            nc.scalar.activation(picked[:], rows[:].indirect(n2_l[:]), ACT.Copy)
+            b_rows.append(rows)
+            b_picked.append(picked)
+
+        ds = [tile([P, H], F32, f"ds{t}") for t in range(PACK)]
+        a_picked = [tile([P, W], F32, f"a_picked{t}") for t in range(PACK)]
+        z2_planes = tile([P, PACK * H], BF16, "z2_planes")
+        ra = [tile([P, W], F32, "ra0")[:], tile([P, W], F32, "ra1")[:], b_rows[PACK - 1][:, 0:W], z2_planes[:].bitcast(F32)[:, 0:W]]
+
+        def fetch_a(t):
+            nc.vector.tensor_copy(ds[t][:], banks[PACK + t][:])
+            nc.scalar.activation(a_picked[t][:], ds[t][:].indirect(n1_l[:]), ACT.Copy)
+
+        def mix(t):
+            nc.vector.scalar_tensor_tensor(ra[t], a_picked[t][:], -0.5, b_picked[t][:], ALU.mult, ALU.add)
+            nc.scalar.activation(ds[t][:].indirect(n1_l[:]), ra[t], ACT.Copy)
+
+        fetch_a(0)
+        fetch_a(1)
+        mix(0)
+        fetch_a(2)
+        mix(1)
+        fetch_a(3)
+
+        nc.tensor.transpose(banks[PACK][:, 0:P], gain_rows[:], identity[:])
+        gains = tile([P, 2 * PACK], F32, "gains")
+        nc.vector.tensor_copy(gains[:], banks[PACK][:, 0 : 2 * PACK])
+        gt_t, gi_t = gains[:, 0:PACK], gains[:, PACK : 2 * PACK]
+
+        for t in range(PACK):
+            nc.vector.tensor_scalar(z2_planes[:, t * H : (t + 1) * H], b_rows[t][:], gi_t[:, t : t + 1], None, ALU.mult)
+        mix(2)
+        z2_grouped = tile([P, H * PACK], BF16, "z2_grouped")
+        nc.vector.tensor_copy(
+            z2_grouped[:].rearrange("p (c i t) -> p c t i", i=4, t=PACK),
+            z2_planes[:].rearrange("p (t c i) -> p c t i", i=4, t=PACK),
+        )
+        mix(3)
+        z2_codes, z2_scales = tile([P, H], U32, "z2_codes"), tile([P, H], U8, "z2_scales")
+        quantize(z2_codes, z2_scales, slice(0, H), z2_grouped[:])
+
+        early = PACK - 1
+        z_planes = tile([P, early, H], BF16, "z_planes")
+        for t in range(early):
+            nc.vector.tensor_scalar(
+                z_planes[:, t, :].rearrange("p (u m) -> p m u", u=PACK),
+                ds[t][:].rearrange("p (m u) -> p m u", u=PACK),
+                gt_t[:, t : t + 1], None, ALU.mult,
+            )
+        z_grouped = tile([P, H, PACK], BF16, "z_grouped")
+        nc.vector.tensor_copy(
+            z_grouped[:, :, 0:early].rearrange("p (c i) t -> p c t i", i=4),
+            z_planes[:].rearrange("p t (c i) -> p c t i", i=4),
+        )
+        z_codes, z_scales = tile([P, H], U32, "z_codes"), tile([P, H], U8, "z_scales")
+        out_rows = out.rearrange("(p u) c -> p u c", u=PACK)
+        list_halves = [slice(0, HALF // 16), slice(HALF // 16, H // 16)]
+        cv = [tile([P, H], F32, f"cv{u}") for u in range(PACK)]
+        size = [tile([P, H], F32, f"size{u}") for u in range(PACK)]
+        root = [tile([P, H], F32, f"root{u}") for u in range(PACK)]
+        inv = [tile([P, H], F32, f"inv{u}") for u in range(PACK)]
+        den = [tile([P, H], F32, f"den{u}") for u in range(PACK)]
+        size4 = [den[0] if u == 2 else tile([P, H], F32, f"size4_{u}") for u in range(PACK)]
+        cv3 = [tile([P, H], F32, "cv3_0")] + den[1:]
+
+        def last_plane(u):
+            cols = slice(u * P, (u + 1) * P)
+            nc.vector.tensor_scalar(z_grouped[:, cols, early], ds[early][:, u::PACK], gt_t[:, early : early + 1], None, ALU.mult)
+
+        def moments(u):
+            cols = slice(u * P, (u + 1) * P)
+            quantize(z_codes, z_scales, cols, z_grouped[:, cols, :].rearrange("p c t -> p (c t)"))
+            product(banks[u], z_codes, z_scales, u, z2_codes, z2_scales)
+
+        def copy_values(u):
+            nc.vector.tensor_scalar(cv[u][:], banks[u][:], 0.0625, None, ALU.mult)
+
+        def take_sizes(u):
+            nc.vector.scalar_tensor_tensor(size[u][:], banks[u][:], -0.0625, cv[u][:], ALU.mult, ALU.max)
+
+        def fetch(dst, src, lst):
+            for h in range(2):
+                nc.scalar.activation(dst[:, halves[h]], src[:].indirect(lst[:, list_halves[h]]), ACT.Copy)
+
+        def inverse_root(u):
+            nc.vector.tensor_tensor(den[u][:], size4[u][:], size[u][:], ALU.add)
+            nc.scalar.activation(root[u][:], den[u][:], ACT.Abs_reciprocal_sqrt, bias=0.5)
+
+        def square(u):
+            nc.vector.tensor_tensor(inv[u][:], root[u][:], root[u][:], ALU.mult)
+
+        def finish(u):
+            res = tile([P, H], F32, f"res{u}")
+            for cols in halves if u == PACK - 1 else [slice(0, H)]:
+                nc.vector.tensor_tensor(res[:, cols], cv3[u][:, cols], inv[u][:, cols], ALU.mult)
+                nc.sync.dma_start(out_rows[:, u, cols], res[:, cols])
+
+        last_plane(0)
+        last_plane(1)
+        moments(0)
+        moments(1)
+        nc.scalar.activation(size[0][:], banks[0][:], ACT.Abs, scale=0.0625)
+        fetch(size4[0], size[0], n4_l)
+        last_plane(2)
+        last_plane(3)
+        moments(2)
+        copy_values(0)
+        fetch(cv3[0], cv[0], n3_l)
+        copy_values(1)
+        moments(3)
+        take_sizes(1)
+        fetch(size4[1], size[1], n4_l)
+        copy_values(2)
+        inverse_root(0)
+        take_sizes(2)
+        fetch(size4[2], size[2], n4_l)
+        inverse_root(1)
+        fetch(cv3[1], cv[1], n3_l)
+        copy_values(3)
+        square(0)
+        take_sizes(3)
+        fetch(size4[3], size[3], n4_l)
+        finish(0)
+        inverse_root(2)
+        fetch(cv3[2], cv[2], n3_l)
+        square(1)
+        finish(1)
+        inverse_root(3)
+        fetch(cv3[3], cv[3], n3_l)
+        square(2)
+        finish(2)
+        square(3)
+        finish(3)

@@ -37,6 +37,10 @@ def tile_picked_momtputbnorm2_none_p_kernel(tc, x_words, x_scales, wa, wb, gt, g
 
         banks = [psum.tile([P, H], F32, name=f"bank{i}") for i in range(8)]
 
+        warm = tile([P, 2], F32, "warm")
+        nc.vector.memset(warm[:, 0:1], 1.0)
+        nc.scalar.activation(warm[:, 1:2], warm[:, 0:1], ACT.Abs_reciprocal_sqrt, bias=0.5)
+
         table_scales = tile([P, T], U8, "table_scales")
         nc.gpsimd.memset(table_scales[:].bitcast(I32), 0)
         for quad in range(4):
@@ -95,11 +99,11 @@ def tile_picked_momtputbnorm2_none_p_kernel(tc, x_words, x_scales, wa, wb, gt, g
         def quantize(codes, scales, cols, values):
             nc.vector.quantize_mx(out=codes[:, cols].bitcast(FP8X4), scales=scales[:, cols], in_=values)
 
-        def product(bank, l_codes, l_scales, block, r_codes, r_scales):
+        def product(bank, l_codes, l_scales, block, r_codes, r_scales, r_cols=slice(0, H)):
             cols = slice(block * P, (block + 1) * P)
             nc.tensor.matmul_mx(
-                out=bank[:], lhsT=l_codes[:, cols].bitcast(FP8X4), lhsT_scale=l_scales[:, cols],
-                rhs=r_codes[:].bitcast(FP8X4), rhs_scale=r_scales[:], start=True, stop=True,
+                out=bank[:, r_cols], lhsT=l_codes[:, cols].bitcast(FP8X4), lhsT_scale=l_scales[:, cols],
+                rhs=r_codes[:, r_cols].bitcast(FP8X4), rhs_scale=r_scales[:, r_cols], start=True, stop=True,
             )
 
         two_scales = pick_scales(two_l, "two_scales")
@@ -130,7 +134,7 @@ def tile_picked_momtputbnorm2_none_p_kernel(tc, x_words, x_scales, wa, wb, gt, g
         ds = [tile([P, H], F32, f"ds{t}") for t in range(PACK)]
         a_picked = [tile([P, W], F32, f"a_picked{t}") for t in range(PACK)]
         z2_planes = tile([P, PACK * H], BF16, "z2_planes")
-        ra = [tile([P, W], F32, "ra0")[:], tile([P, W], F32, "ra1")[:], b_rows[PACK - 1][:, 0:W], z2_planes[:].bitcast(F32)[:, 0:W]]
+        ra = [tile([P, W], F32, f"ra{t}")[:] for t in range(PACK)]
 
         def fetch_a(t):
             nc.vector.tensor_copy(ds[t][:], banks[PACK + t][:])
@@ -140,12 +144,10 @@ def tile_picked_momtputbnorm2_none_p_kernel(tc, x_words, x_scales, wa, wb, gt, g
             nc.vector.scalar_tensor_tensor(ra[t], a_picked[t][:], -0.5, b_picked[t][:], ALU.mult, ALU.add)
             nc.scalar.activation(ds[t][:].indirect(n1_l[:]), ra[t], ACT.Copy)
 
-        fetch_a(0)
-        fetch_a(1)
-        mix(0)
-        fetch_a(2)
-        mix(1)
-        fetch_a(3)
+        for t in range(PACK):
+            fetch_a(t)
+        for t in range(PACK):
+            mix(t)
 
         nc.tensor.transpose(banks[PACK][:, 0:P], gain_rows[:], identity[:])
         gains = tile([P, 2 * PACK], F32, "gains")
@@ -154,13 +156,11 @@ def tile_picked_momtputbnorm2_none_p_kernel(tc, x_words, x_scales, wa, wb, gt, g
 
         for t in range(PACK):
             nc.vector.tensor_scalar(z2_planes[:, t * H : (t + 1) * H], b_rows[t][:], gi_t[:, t : t + 1], None, ALU.mult)
-        mix(2)
         z2_grouped = tile([P, H * PACK], BF16, "z2_grouped")
         nc.vector.tensor_copy(
             z2_grouped[:].rearrange("p (c i t) -> p c t i", i=4, t=PACK),
             z2_planes[:].rearrange("p (t c i) -> p c t i", i=4, t=PACK),
         )
-        mix(3)
         z2_codes, z2_scales = tile([P, H], U32, "z2_codes"), tile([P, H], U8, "z2_scales")
         quantize(z2_codes, z2_scales, slice(0, H), z2_grouped[:])
 
@@ -179,7 +179,7 @@ def tile_picked_momtputbnorm2_none_p_kernel(tc, x_words, x_scales, wa, wb, gt, g
         )
         z_codes, z_scales = tile([P, H], U32, "z_codes"), tile([P, H], U8, "z_scales")
         out_rows = out.rearrange("(p u) c -> p u c", u=PACK)
-        list_halves = [slice(0, HALF // 16), slice(HALF // 16, H // 16)]
+        last_pieces = [slice(0, HALF), slice(HALF, HALF + P), slice(HALF + P, H)]
         cv = [tile([P, H], F32, f"cv{u}") for u in range(PACK)]
         size = [tile([P, H], F32, f"size{u}") for u in range(PACK)]
         root = [tile([P, H], F32, f"root{u}") for u in range(PACK)]
@@ -188,6 +188,8 @@ def tile_picked_momtputbnorm2_none_p_kernel(tc, x_words, x_scales, wa, wb, gt, g
         size4 = [den[0] if u == 2 else tile([P, H], F32, f"size4_{u}") for u in range(PACK)]
         cv3 = [tile([P, H], F32, "cv3_0")] + den[1:]
 
+        first_banks = [banks[0], banks[PACK + 1]]
+
         def last_plane(u):
             cols = slice(u * P, (u + 1) * P)
             nc.vector.tensor_scalar(z_grouped[:, cols, early], ds[early][:, u::PACK], gt_t[:, early : early + 1], None, ALU.mult)
@@ -195,7 +197,11 @@ def tile_picked_momtputbnorm2_none_p_kernel(tc, x_words, x_scales, wa, wb, gt, g
         def moments(u):
             cols = slice(u * P, (u + 1) * P)
             quantize(z_codes, z_scales, cols, z_grouped[:, cols, :].rearrange("p c t -> p (c t)"))
-            product(banks[u], z_codes, z_scales, u, z2_codes, z2_scales)
+            if u == 0:
+                for h in range(2):
+                    product(first_banks[h], z_codes, z_scales, u, z2_codes, z2_scales, halves[h])
+            else:
+                product(banks[u], z_codes, z_scales, u, z2_codes, z2_scales)
 
         def copy_values(u):
             nc.vector.tensor_scalar(cv[u][:], banks[u][:], 0.0625, None, ALU.mult)
@@ -203,9 +209,9 @@ def tile_picked_momtputbnorm2_none_p_kernel(tc, x_words, x_scales, wa, wb, gt, g
         def take_sizes(u):
             nc.vector.scalar_tensor_tensor(size[u][:], banks[u][:], -0.0625, cv[u][:], ALU.mult, ALU.max)
 
-        def fetch(dst, src, lst):
-            for h in range(2):
-                nc.scalar.activation(dst[:, halves[h]], src[:].indirect(lst[:, list_halves[h]]), ACT.Copy)
+        def fetch(dst, src, lst, pieces=halves):
+            for cols in pieces:
+                nc.scalar.activation(dst[:, cols], src[:].indirect(lst[:, cols.start // 16 : cols.stop // 16]), ACT.Copy)
 
         def inverse_root(u):
             nc.vector.tensor_tensor(den[u][:], size4[u][:], size[u][:], ALU.add)
@@ -216,42 +222,41 @@ def tile_picked_momtputbnorm2_none_p_kernel(tc, x_words, x_scales, wa, wb, gt, g
 
         def finish(u):
             res = tile([P, H], F32, f"res{u}")
-            for cols in halves if u == PACK - 1 else [slice(0, H)]:
+            for cols in last_pieces if u == PACK - 1 else [slice(0, H)]:
                 nc.vector.tensor_tensor(res[:, cols], cv3[u][:, cols], inv[u][:, cols], ALU.mult)
                 nc.sync.dma_start(out_rows[:, u, cols], res[:, cols])
 
-        last_plane(0)
-        last_plane(1)
-        moments(0)
-        moments(1)
-        nc.scalar.activation(size[0][:], banks[0][:], ACT.Abs, scale=0.0625)
-        fetch(size4[0], size[0], n4_l)
-        last_plane(2)
-        last_plane(3)
-        moments(2)
-        copy_values(0)
+        for pair in range(2):
+            last_plane(2 * pair)
+            last_plane(2 * pair + 1)
+            moments(2 * pair)
+            moments(2 * pair + 1)
+        nc.scalar.activation(cv[0][:, halves[0]], first_banks[0][:, halves[0]], ACT.Copy, scale=0.0625)
+        nc.vector.tensor_scalar(cv[0][:, halves[1]], first_banks[1][:, halves[1]], 0.0625, None, ALU.mult)
         fetch(cv3[0], cv[0], n3_l)
+        for h in range(2):
+            nc.vector.scalar_tensor_tensor(size[0][:, halves[h]], first_banks[h][:, halves[h]], -0.0625, cv[0][:, halves[h]], ALU.mult, ALU.max)
+        fetch(size4[0], size[0], n4_l)
         copy_values(1)
-        moments(3)
+        copy_values(2)
         take_sizes(1)
         fetch(size4[1], size[1], n4_l)
-        copy_values(2)
-        inverse_root(0)
         take_sizes(2)
+        inverse_root(0)
         fetch(size4[2], size[2], n4_l)
+        copy_values(3)
         inverse_root(1)
         fetch(cv3[1], cv[1], n3_l)
-        copy_values(3)
-        square(0)
         take_sizes(3)
         fetch(size4[3], size[3], n4_l)
-        finish(0)
+        square(0)
         inverse_root(2)
         fetch(cv3[2], cv[2], n3_l)
+        finish(0)
         square(1)
         finish(1)
         inverse_root(3)
-        fetch(cv3[3], cv[3], n3_l)
+        fetch(cv3[3], cv[3], n3_l, last_pieces)
         square(2)
         finish(2)
         square(3)

@@ -37,14 +37,13 @@ def tile_picked_momtputbnorm2_none_p_kernel(tc, x_words, x_scales, wa, wb, gt, g
 
         banks = [psum.tile([P, H], F32, name=f"bank{i}") for i in range(8)]
 
-        warm = tile([P, 2], F32, "warm")
-        nc.vector.memset(warm[:, 0:1], 1.0)
-        nc.scalar.activation(warm[:, 1:2], warm[:, 0:1], ACT.Abs_reciprocal_sqrt, bias=0.5)
-
         table_scales = tile([P, T], U8, "table_scales")
         nc.gpsimd.memset(table_scales[:].bitcast(I32), 0)
         for quad in range(4):
-            nc.sync.dma_start(table_scales[32 * quad : 32 * quad + 4, :].bitcast(I32), x_scales[0, 4 * quad : 4 * quad + 4, :].bitcast(I32))
+            (nc.sync if quad < 2 else nc.scalar).dma_start(table_scales[32 * quad : 32 * quad + 4, :].bitcast(I32), x_scales[0, 4 * quad : 4 * quad + 4, :].bitcast(I32))
+        warm_in, warm_out = tile([P, 1], F32, "warm_in"), tile([P, 1], F32, "warm_out")
+        nc.gpsimd.memset(warm_in[:], 1.0)
+        nc.scalar.activation(warm_out[:], warm_in[:], ACT.Abs_reciprocal_sqrt, bias=0.5)
         two_l = load_list(two, "two_l")
         offs_l = load_list(offs, "offs_l")
         table_words = tile([P, T], U32, "table_words")
@@ -122,17 +121,16 @@ def tile_picked_momtputbnorm2_none_p_kernel(tc, x_words, x_scales, wa, wb, gt, g
         for t in range(PACK):
             product(banks[PACK + t], offs_words, offs_scales, t, wa_codes, wa_scales)
 
-        b_rows, b_picked = [], []
+        cv_wide = [tile([P, 2 * H if u < PACK - 1 else H], F32, f"cv_wide{u}") for u in range(PACK)]
+        size_wide = [tile([P, 2 * H], F32, f"size_wide{u}") for u in range(PACK)]
+        b_rows = [cv_wide[t][:, H:] for t in range(PACK - 1)] + [tile([P, H], F32, "b_last")[:]]
+        b_picked = [size_wide[t][:, H : H + W] for t in range(PACK)]
+        a_picked = [size_wide[t][:, H + W :] for t in range(PACK)]
         for t in range(PACK):
-            rows = tile([P, H], F32, f"b_rows{t}")
-            nc.vector.tensor_copy(rows[:], banks[t][:])
-            picked = tile([P, W], F32, f"b_picked{t}")
-            nc.scalar.activation(picked[:], rows[:].indirect(n2_l[:]), ACT.Copy)
-            b_rows.append(rows)
-            b_picked.append(picked)
+            nc.vector.tensor_copy(b_rows[t], banks[t][:])
+            nc.scalar.activation(b_picked[t], b_rows[t].indirect(n2_l[:]), ACT.Copy)
 
         ds = [tile([P, H], F32, f"ds{t}") for t in range(PACK)]
-        a_picked = [tile([P, W], F32, f"a_picked{t}") for t in range(PACK)]
         z2_planes = tile([P, PACK * H], BF16, "z2_planes")
         ra = [tile([P, W], F32, f"ra{t}")[:] for t in range(PACK)]
 
@@ -165,23 +163,18 @@ def tile_picked_momtputbnorm2_none_p_kernel(tc, x_words, x_scales, wa, wb, gt, g
         quantize(z2_codes, z2_scales, slice(0, H), z2_grouped[:])
 
         early = PACK - 1
-        z_planes = tile([P, early, H], BF16, "z_planes")
+        z_grouped = tile([P, H, PACK], BF16, "z_grouped")
         for t in range(early):
             nc.vector.tensor_scalar(
-                z_planes[:, t, :].rearrange("p (u m) -> p m u", u=PACK),
+                z_grouped[:, :, t].rearrange("p (u m) -> p m u", u=PACK),
                 ds[t][:].rearrange("p (m u) -> p m u", u=PACK),
                 gt_t[:, t : t + 1], None, ALU.mult,
             )
-        z_grouped = tile([P, H, PACK], BF16, "z_grouped")
-        nc.vector.tensor_copy(
-            z_grouped[:, :, 0:early].rearrange("p (c i) t -> p c t i", i=4),
-            z_planes[:].rearrange("p t (c i) -> p c t i", i=4),
-        )
         z_codes, z_scales = tile([P, H], U32, "z_codes"), tile([P, H], U8, "z_scales")
         out_rows = out.rearrange("(p u) c -> p u c", u=PACK)
         last_pieces = [slice(0, HALF), slice(HALF, HALF + P), slice(HALF + P, H)]
-        cv = [tile([P, H], F32, f"cv{u}") for u in range(PACK)]
-        size = [tile([P, H], F32, f"size{u}") for u in range(PACK)]
+        cv = [cv_wide[u][:, 0:H] for u in range(PACK)]
+        size = [size_wide[u][:, 0:H] for u in range(PACK)]
         root = [tile([P, H], F32, f"root{u}") for u in range(PACK)]
         inv = [tile([P, H], F32, f"inv{u}") for u in range(PACK)]
         den = [tile([P, H], F32, f"den{u}") for u in range(PACK)]
@@ -209,7 +202,7 @@ def tile_picked_momtputbnorm2_none_p_kernel(tc, x_words, x_scales, wa, wb, gt, g
         def take_sizes(u):
             nc.vector.scalar_tensor_tensor(size[u][:], banks[u][:], -0.0625, cv[u][:], ALU.mult, ALU.max)
 
-        def fetch(dst, src, lst, pieces=halves):
+        def fetch(dst, src, lst, pieces=(slice(0, H),)):
             for cols in pieces:
                 nc.scalar.activation(dst[:, cols], src[:].indirect(lst[:, cols.start // 16 : cols.stop // 16]), ACT.Copy)
 
@@ -233,30 +226,30 @@ def tile_picked_momtputbnorm2_none_p_kernel(tc, x_words, x_scales, wa, wb, gt, g
             moments(2 * pair + 1)
         nc.scalar.activation(cv[0][:, halves[0]], first_banks[0][:, halves[0]], ACT.Copy, scale=0.0625)
         nc.vector.tensor_scalar(cv[0][:, halves[1]], first_banks[1][:, halves[1]], 0.0625, None, ALU.mult)
-        fetch(cv3[0], cv[0], n3_l)
+        fetch(cv3[0], cv_wide[0], n3_l)
         for h in range(2):
             nc.vector.scalar_tensor_tensor(size[0][:, halves[h]], first_banks[h][:, halves[h]], -0.0625, cv[0][:, halves[h]], ALU.mult, ALU.max)
-        fetch(size4[0], size[0], n4_l)
+        fetch(size4[0], size_wide[0], n4_l)
         copy_values(1)
         copy_values(2)
         take_sizes(1)
-        fetch(size4[1], size[1], n4_l)
+        fetch(size4[1], size_wide[1], n4_l)
         take_sizes(2)
         inverse_root(0)
-        fetch(size4[2], size[2], n4_l)
+        fetch(size4[2], size_wide[2], n4_l)
         copy_values(3)
         inverse_root(1)
-        fetch(cv3[1], cv[1], n3_l)
+        fetch(cv3[1], cv_wide[1], n3_l)
         take_sizes(3)
-        fetch(size4[3], size[3], n4_l)
+        fetch(size4[3], size_wide[3], n4_l)
         square(0)
         inverse_root(2)
-        fetch(cv3[2], cv[2], n3_l)
+        fetch(cv3[2], cv_wide[2], n3_l)
         finish(0)
         square(1)
         finish(1)
         inverse_root(3)
-        fetch(cv3[3], cv[3], n3_l, last_pieces)
+        fetch(cv3[3], cv_wide[3], n3_l, last_pieces)
         square(2)
         finish(2)
         square(3)

@@ -41,6 +41,13 @@ def tile_picked_momtputbnorm2_none_p_kernel(tc, x_words, x_scales, wa, wb, gt, g
         nc.gpsimd.memset(table_scales[:].bitcast(I32), 0)
         for quad in range(4):
             (nc.sync if quad < 2 else nc.scalar).dma_start(table_scales[32 * quad : 32 * quad + 4, :].bitcast(I32), x_scales[0, 4 * quad : 4 * quad + 4, :].bitcast(I32))
+        gain_rows = tile([P, P], F32, "gain_rows")
+        nc.gpsimd.memset(gain_rows[:], 0.0)
+        for first, src in ((0, gt), (PACK, gi)):
+            nc.scalar.dma_start(
+                gain_rows[first : first + PACK, :].rearrange("t (q r) -> t q r", r=8),
+                src.rearrange("(q t r) o -> t q (r o)", t=PACK, r=8),
+            )
         warm_in, warm_out = tile([P, 1], F32, "warm_in"), tile([P, 1], F32, "warm_out")
         nc.gpsimd.memset(warm_in[:], 1.0)
         nc.scalar.activation(warm_out[:], warm_in[:], ACT.Abs_reciprocal_sqrt, bias=0.5)
@@ -62,15 +69,12 @@ def tile_picked_momtputbnorm2_none_p_kernel(tc, x_words, x_scales, wa, wb, gt, g
         n1_l = load_list(n1, "n1_l")
         n4_l = load_list(n4, "n4_l")
         n3_l = load_list(n3, "n3_l")
-        gain_rows = tile([P, P], F32, "gain_rows")
-        nc.gpsimd.memset(gain_rows[:], 0.0)
-        for first, src in ((0, gt), (PACK, gi)):
-            nc.gpsimd.dma_start(
-                gain_rows[first : first + PACK, :].rearrange("t (q r) -> t q r", r=8),
-                src.rearrange("(q t r) o -> t q (r o)", t=PACK, r=8),
-            )
         identity = tile([P, P], F32, "identity")
         make_identity(nc, identity[:])
+        nc.tensor.transpose(banks[7][:, 0:P], gain_rows[:], identity[:])
+        gains = tile([P, 2 * PACK], F32, "gains")
+        nc.scalar.copy(gains[:], banks[7][:, 0 : 2 * PACK])
+        gt_t, gi_t = gains[:, 0:PACK], gains[:, PACK : 2 * PACK]
 
         def pick_scales(lst, name):
             picked = tile([P, S], U8, name + "_picked")
@@ -87,10 +91,9 @@ def tile_picked_momtputbnorm2_none_p_kernel(tc, x_words, x_scales, wa, wb, gt, g
             nc.vector.tensor_copy(picked[:].rearrange("p (t q r) -> p q t r", t=PACK, r=8), table_words[:].indirect(lst[:]))
             return picked
 
-        def round_weights(raw, name):
-            grouped = tile([P, HALF * PACK], BF16, name)
+        def round_weights(raw, grouped):
             nc.scalar.copy(
-                grouped[:].rearrange("p (c i j) -> p c j i", i=4, j=PACK),
+                grouped.rearrange("p (c i j) -> p c j i", i=4, j=PACK),
                 raw[:].rearrange("p j (c i) -> p c j i", i=4),
             )
             return grouped
@@ -113,11 +116,11 @@ def tile_picked_momtputbnorm2_none_p_kernel(tc, x_words, x_scales, wa, wb, gt, g
         wb_codes, wb_scales = tile([P, H], U32, "wb_codes"), tile([P, H], U8, "wb_scales")
         wa_codes, wa_scales = tile([P, H], U32, "wa_codes"), tile([P, H], U8, "wa_scales")
         for h in range(2):
-            quantize(wb_codes, wb_scales, halves[h], round_weights(wb_raw[h], f"wb_grouped{h}")[:])
+            quantize(wb_codes, wb_scales, halves[h], round_weights(wb_raw[h], tile([P, HALF * PACK], BF16, f"wb_grouped{h}")[:]))
         for t in range(PACK):
             product(banks[t], two_words, two_scales, t, wb_codes, wb_scales)
         for h in range(2):
-            quantize(wa_codes, wa_scales, halves[h], round_weights(wa_raw[h], f"wa_grouped{h}")[:])
+            quantize(wa_codes, wa_scales, halves[h], round_weights(wa_raw[h], tile([P, HALF * PACK], BF16, f"wa_grouped{h}")[:]))
         for t in range(PACK):
             product(banks[PACK + t], offs_words, offs_scales, t, wa_codes, wa_scales)
 
@@ -131,7 +134,6 @@ def tile_picked_momtputbnorm2_none_p_kernel(tc, x_words, x_scales, wa, wb, gt, g
             nc.scalar.activation(b_picked[t], b_rows[t].indirect(n2_l[:]), ACT.Copy)
 
         ds = [tile([P, H], F32, f"ds{t}") for t in range(PACK)]
-        z2_planes = tile([P, PACK * H], BF16, "z2_planes")
         ra = [tile([P, W], F32, f"ra{t}")[:] for t in range(PACK)]
 
         def fetch_a(t):
@@ -147,11 +149,7 @@ def tile_picked_momtputbnorm2_none_p_kernel(tc, x_words, x_scales, wa, wb, gt, g
         for t in range(PACK):
             mix(t)
 
-        nc.tensor.transpose(banks[PACK][:, 0:P], gain_rows[:], identity[:])
-        gains = tile([P, 2 * PACK], F32, "gains")
-        nc.vector.tensor_copy(gains[:], banks[PACK][:, 0 : 2 * PACK])
-        gt_t, gi_t = gains[:, 0:PACK], gains[:, PACK : 2 * PACK]
-
+        z2_planes = tile([P, PACK * H], BF16, "z2_planes")
         for t in range(PACK):
             nc.vector.tensor_scalar(z2_planes[:, t * H : (t + 1) * H], b_rows[t][:], gi_t[:, t : t + 1], None, ALU.mult)
         z2_grouped = tile([P, H * PACK], BF16, "z2_grouped")
@@ -178,8 +176,8 @@ def tile_picked_momtputbnorm2_none_p_kernel(tc, x_words, x_scales, wa, wb, gt, g
         root = [tile([P, H], F32, f"root{u}") for u in range(PACK)]
         inv = [tile([P, H], F32, f"inv{u}") for u in range(PACK)]
         den = [tile([P, H], F32, f"den{u}") for u in range(PACK)]
-        size4 = [den[0] if u == 2 else tile([P, H], F32, f"size4_{u}") for u in range(PACK)]
-        cv3 = [tile([P, H], F32, "cv3_0")] + den[1:]
+        size4 = [tile([P, H], F32, f"size4_{u}") for u in range(PACK)]
+        cv3 = [tile([P, H], F32, "cv3_0")] + den[:-1]
 
         first_banks = [banks[0], banks[PACK + 1]]
 
@@ -232,25 +230,21 @@ def tile_picked_momtputbnorm2_none_p_kernel(tc, x_words, x_scales, wa, wb, gt, g
         fetch(size4[0], size_wide[0], n4_l)
         copy_values(1)
         copy_values(2)
-        take_sizes(1)
-        fetch(size4[1], size_wide[1], n4_l)
-        take_sizes(2)
-        inverse_root(0)
-        fetch(size4[2], size_wide[2], n4_l)
+        for u in (1, 2):
+            take_sizes(u)
+            fetch(size4[u], size_wide[u], n4_l)
         copy_values(3)
-        inverse_root(1)
-        fetch(cv3[1], cv_wide[1], n3_l)
+        inverse_root(0)
         take_sizes(3)
         fetch(size4[3], size_wide[3], n4_l)
-        square(0)
+        inverse_root(1)
+        fetch(cv3[1], cv_wide[1], n3_l)
         inverse_root(2)
         fetch(cv3[2], cv_wide[2], n3_l)
-        finish(0)
-        square(1)
-        finish(1)
+        square(0)
         inverse_root(3)
         fetch(cv3[3], cv_wide[3], n3_l, last_pieces)
-        square(2)
-        finish(2)
-        square(3)
-        finish(3)
+        finish(0)
+        for u in range(1, PACK):
+            square(u)
+            finish(u)

@@ -16,7 +16,15 @@ ACT = mybir.ActivationFunctionType
 K, T, S, H, W = 512, 2048, 512, 512, 256
 P = 128
 PACK = 4
+LAST = PACK - 1
+RUN = 8
+LINE = 4
+LIST_ROWS = 16
 HALF = H // 2
+HALVES = [slice(0, HALF), slice(HALF, H)]
+ALL = slice(0, H)
+LAST_PIECES = [slice(0, HALF), slice(HALF, HALF + P), slice(HALF + P, H)]
+CV_SCALE = 0.0625
 FLOPS = 2 * (2 * K * S * H + S * H * H)
 
 
@@ -28,39 +36,35 @@ def tile_picked_momtputbnorm2_none_p_kernel(tc, x_words, x_scales, wa, wb, gt, g
         psum = ctx.enter_context(tc.psum_pool(name="psum", bufs=1))
 
         def load_list(src, name):
-            tile = lists.tile(list(src.shape), U16, name=name)
-            nc.sync.dma_start(tile[:], src)
-            return tile
+            offsets = lists.tile(list(src.shape), U16, name=name)
+            nc.sync.dma_start(offsets[:], src)
+            return offsets
 
         def tile(shape, dtype, name):
             return sb.tile(shape, dtype, name=name, align_bytes=64)
 
-        banks = [psum.tile([P, H], F32, name=f"bank{i}") for i in range(8)]
+        banks = [psum.tile([P, H], F32, name=f"bank{i}") for i in range(2 * PACK)]
+        b_banks, a_banks = banks[:PACK], banks[PACK:]
 
         table_scales = tile([P, T], U8, "table_scales")
         nc.gpsimd.memset(table_scales[:].bitcast(I32), 0)
         for quad in range(4):
-            (nc.sync if quad < 2 else nc.scalar).dma_start(table_scales[32 * quad : 32 * quad + 4, :].bitcast(I32), x_scales[0, 4 * quad : 4 * quad + 4, :].bitcast(I32))
-        gain_rows = tile([P, P], F32, "gain_rows")
-        nc.gpsimd.memset(gain_rows[:], 0.0)
-        for first, src in ((0, gt), (PACK, gi)):
-            nc.scalar.dma_start(
-                gain_rows[first : first + PACK, :].rearrange("t (q r) -> t q r", r=8),
-                src.rearrange("(q t r) o -> t q (r o)", t=PACK, r=8),
-            )
+            queue = nc.sync if quad < 2 else nc.scalar
+            queue.dma_start(table_scales[32 * quad : 32 * quad + 4, :].bitcast(I32), x_scales[0, 4 * quad : 4 * quad + 4, :].bitcast(I32))
+
         warm_in, warm_out = tile([P, 1], F32, "warm_in"), tile([P, 1], F32, "warm_out")
         nc.gpsimd.memset(warm_in[:], 1.0)
         nc.scalar.activation(warm_out[:], warm_in[:], ACT.Abs_reciprocal_sqrt, bias=0.5)
+
         two_l = load_list(two, "two_l")
         offs_l = load_list(offs, "offs_l")
         table_words = tile([P, T], U32, "table_words")
         nc.sync.dma_start(table_words[:].bitcast(I32), x_words[0].rearrange("p n j -> p (n j)").bitcast(I32))
-        halves = [slice(0, HALF), slice(HALF, H)]
 
         def load_weights(w, name):
             raws = [tile([P, PACK, HALF], F32, f"{name}{h}") for h in range(2)]
             for h in range(2):
-                nc.sync.dma_start(raws[h][:], w.rearrange("(p j) c -> p j c", j=PACK)[:, :, halves[h]])
+                nc.sync.dma_start(raws[h][:], w.rearrange("(p j) c -> p j c", j=PACK)[:, :, HALVES[h]])
             return raws
 
         wb_raw = load_weights(wb, "wb_raw")
@@ -69,42 +73,47 @@ def tile_picked_momtputbnorm2_none_p_kernel(tc, x_words, x_scales, wa, wb, gt, g
         n1_l = load_list(n1, "n1_l")
         n4_l = load_list(n4, "n4_l")
         n3_l = load_list(n3, "n3_l")
+
+        gain_rows = tile([P, P], F32, "gain_rows")
+        nc.gpsimd.memset(gain_rows[:], 0.0)
+        for first, src in ((0, gt), (PACK, gi)):
+            nc.gpsimd.dma_start(
+                gain_rows[first : first + PACK, :].rearrange("t (q r) -> t q r", r=RUN),
+                src.rearrange("(q t r) o -> t q (r o)", t=PACK, r=RUN),
+            )
         identity = tile([P, P], F32, "identity")
         make_identity(nc, identity[:])
-        nc.tensor.transpose(banks[7][:, 0:P], gain_rows[:], identity[:])
-        gains = tile([P, 2 * PACK], F32, "gains")
-        nc.scalar.copy(gains[:], banks[7][:, 0 : 2 * PACK])
-        gt_t, gi_t = gains[:, 0:PACK], gains[:, PACK : 2 * PACK]
 
-        def pick_scales(lst, name):
+        def pick_scales(offsets, name):
             picked = tile([P, S], U8, name + "_picked")
-            nc.vector.tensor_copy(picked[:], table_scales[:].indirect(lst[:]))
+            nc.vector.tensor_copy(picked[:], table_scales[:].indirect(offsets[:]))
             dealt = tile([P, S], U8, name + "_dealt")
             nc.vector.tensor_copy(
-                dealt[:].bitcast(I32).rearrange("p (t q w) -> p t q w", t=PACK, w=2),
-                picked[:].bitcast(I32).rearrange("p (q t w) -> p t q w", t=PACK, w=2),
+                dealt[:].bitcast(I32).rearrange("p (t q w) -> p t q w", t=PACK, w=RUN // 4),
+                picked[:].bitcast(I32).rearrange("p (q t w) -> p t q w", t=PACK, w=RUN // 4),
             )
             return dealt
 
-        def pick_words(lst, name):
+        def pick_words(offsets, name):
             picked = tile([P, S], U32, name)
-            nc.vector.tensor_copy(picked[:].rearrange("p (t q r) -> p q t r", t=PACK, r=8), table_words[:].indirect(lst[:]))
+            nc.vector.tensor_copy(picked[:].rearrange("p (t q r) -> p q t r", t=PACK, r=RUN), table_words[:].indirect(offsets[:]))
             return picked
 
-        def round_weights(raw, grouped):
+        def round_weights(raw, name):
+            grouped = tile([P, HALF * PACK], BF16, name)
             nc.scalar.copy(
-                grouped.rearrange("p (c i j) -> p c j i", i=4, j=PACK),
-                raw[:].rearrange("p j (c i) -> p c j i", i=4),
+                grouped[:].rearrange("p (c i j) -> p c j i", i=LINE, j=PACK),
+                raw[:].rearrange("p j (c i) -> p c j i", i=LINE),
             )
             return grouped
 
         def quantize(codes, scales, cols, values):
             nc.vector.quantize_mx(out=codes[:, cols].bitcast(FP8X4), scales=scales[:, cols], in_=values)
 
-        def product(bank, l_codes, l_scales, block, r_codes, r_scales, r_cols=slice(0, H)):
-            cols = slice(block * P, (block + 1) * P)
+        def product(bank, l_codes, l_scales, block, r_codes, r_scales, r_cols=ALL):
+            l_cols = slice(block * P, (block + 1) * P)
             nc.tensor.matmul_mx(
-                out=bank[:, r_cols], lhsT=l_codes[:, cols].bitcast(FP8X4), lhsT_scale=l_scales[:, cols],
+                out=bank[:, r_cols], lhsT=l_codes[:, l_cols].bitcast(FP8X4), lhsT_scale=l_scales[:, l_cols],
                 rhs=r_codes[:, r_cols].bitcast(FP8X4), rhs_scale=r_scales[:, r_cols], start=True, stop=True,
             )
 
@@ -116,134 +125,132 @@ def tile_picked_momtputbnorm2_none_p_kernel(tc, x_words, x_scales, wa, wb, gt, g
         wb_codes, wb_scales = tile([P, H], U32, "wb_codes"), tile([P, H], U8, "wb_scales")
         wa_codes, wa_scales = tile([P, H], U32, "wa_codes"), tile([P, H], U8, "wa_scales")
         for h in range(2):
-            quantize(wb_codes, wb_scales, halves[h], round_weights(wb_raw[h], tile([P, HALF * PACK], BF16, f"wb_grouped{h}")[:]))
+            quantize(wb_codes, wb_scales, HALVES[h], round_weights(wb_raw[h], f"wb_grouped{h}")[:])
         for t in range(PACK):
-            product(banks[t], two_words, two_scales, t, wb_codes, wb_scales)
+            product(b_banks[t], two_words, two_scales, t, wb_codes, wb_scales)
         for h in range(2):
-            quantize(wa_codes, wa_scales, halves[h], round_weights(wa_raw[h], tile([P, HALF * PACK], BF16, f"wa_grouped{h}")[:]))
+            quantize(wa_codes, wa_scales, HALVES[h], round_weights(wa_raw[h], f"wa_grouped{h}")[:])
         for t in range(PACK):
-            product(banks[PACK + t], offs_words, offs_scales, t, wa_codes, wa_scales)
+            product(a_banks[t], offs_words, offs_scales, t, wa_codes, wa_scales)
 
-        cv_wide = [tile([P, 2 * H if u < PACK - 1 else H], F32, f"cv_wide{u}") for u in range(PACK)]
-        size_wide = [tile([P, 2 * H], F32, f"size_wide{u}") for u in range(PACK)]
-        b_rows = [cv_wide[t][:, H:] for t in range(PACK - 1)] + [tile([P, H], F32, "b_last")[:]]
-        b_picked = [size_wide[t][:, H : H + W] for t in range(PACK)]
-        a_picked = [size_wide[t][:, H + W :] for t in range(PACK)]
+        cv_tiles = [tile([P, 2 * H if u < LAST else H], F32, f"cv_tile{u}") for u in range(PACK)]
+        size_tiles = [tile([P, 2 * H], F32, f"size_tile{u}") for u in range(PACK)]
+        b_rows = [cv_tiles[t][:, H:] for t in range(LAST)] + [tile([P, H], F32, "b_last")[:]]
+        b_picked = [size_tiles[t][:, H : H + W] for t in range(PACK)]
+        a_picked = [size_tiles[t][:, H + W :] for t in range(PACK)]
         for t in range(PACK):
-            nc.vector.tensor_copy(b_rows[t], banks[t][:])
+            nc.vector.tensor_copy(b_rows[t], b_banks[t][:])
             nc.scalar.activation(b_picked[t], b_rows[t].indirect(n2_l[:]), ACT.Copy)
 
         ds = [tile([P, H], F32, f"ds{t}") for t in range(PACK)]
-        ra = [tile([P, W], F32, f"ra{t}")[:] for t in range(PACK)]
-
-        def fetch_a(t):
-            nc.vector.tensor_copy(ds[t][:], banks[PACK + t][:])
-            nc.scalar.activation(a_picked[t][:], ds[t][:].indirect(n1_l[:]), ACT.Copy)
-
-        def mix(t):
-            nc.vector.scalar_tensor_tensor(ra[t], a_picked[t][:], -0.5, b_picked[t][:], ALU.mult, ALU.add)
-            nc.scalar.activation(ds[t][:].indirect(n1_l[:]), ra[t], ACT.Copy)
-
-        for t in range(PACK):
-            fetch_a(t)
-        for t in range(PACK):
-            mix(t)
-
         z2_planes = tile([P, PACK * H], BF16, "z2_planes")
+        ra = [tile([P, W], F32, f"ra{t}") for t in range(PACK)]
         for t in range(PACK):
-            nc.vector.tensor_scalar(z2_planes[:, t * H : (t + 1) * H], b_rows[t][:], gi_t[:, t : t + 1], None, ALU.mult)
+            nc.vector.tensor_copy(ds[t][:], a_banks[t][:])
+            nc.scalar.activation(a_picked[t], ds[t][:].indirect(n1_l[:]), ACT.Copy)
+        for t in range(PACK):
+            nc.vector.scalar_tensor_tensor(ra[t][:], a_picked[t], -0.5, b_picked[t], ALU.mult, ALU.add)
+            nc.scalar.activation(ds[t][:].indirect(n1_l[:]), ra[t][:], ACT.Copy)
+
+        nc.tensor.transpose(a_banks[0][:, 0:P], gain_rows[:], identity[:])
+        gains = tile([P, 2 * PACK], F32, "gains")
+        nc.vector.tensor_copy(gains[:], a_banks[0][:, 0 : 2 * PACK])
+        gt_cols, gi_cols = gains[:, 0:PACK], gains[:, PACK : 2 * PACK]
+
+        for t in range(PACK):
+            nc.vector.tensor_scalar(z2_planes[:, t * H : (t + 1) * H], b_rows[t], gi_cols[:, t : t + 1], None, ALU.mult)
         z2_grouped = tile([P, H * PACK], BF16, "z2_grouped")
         nc.vector.tensor_copy(
-            z2_grouped[:].rearrange("p (c i t) -> p c t i", i=4, t=PACK),
-            z2_planes[:].rearrange("p (t c i) -> p c t i", i=4, t=PACK),
+            z2_grouped[:].rearrange("p (c i t) -> p c t i", i=LINE, t=PACK),
+            z2_planes[:].rearrange("p (t c i) -> p c t i", i=LINE, t=PACK),
         )
         z2_codes, z2_scales = tile([P, H], U32, "z2_codes"), tile([P, H], U8, "z2_scales")
-        quantize(z2_codes, z2_scales, slice(0, H), z2_grouped[:])
+        quantize(z2_codes, z2_scales, ALL, z2_grouped[:])
 
-        early = PACK - 1
         z_grouped = tile([P, H, PACK], BF16, "z_grouped")
-        for t in range(early):
+        for t in range(LAST):
             nc.vector.tensor_scalar(
                 z_grouped[:, :, t].rearrange("p (u m) -> p m u", u=PACK),
                 ds[t][:].rearrange("p (m u) -> p m u", u=PACK),
-                gt_t[:, t : t + 1], None, ALU.mult,
+                gt_cols[:, t : t + 1], None, ALU.mult,
             )
         z_codes, z_scales = tile([P, H], U32, "z_codes"), tile([P, H], U8, "z_scales")
+
         out_rows = out.rearrange("(p u) c -> p u c", u=PACK)
-        last_pieces = [slice(0, HALF), slice(HALF, HALF + P), slice(HALF + P, H)]
-        cv = [cv_wide[u][:, 0:H] for u in range(PACK)]
-        size = [size_wide[u][:, 0:H] for u in range(PACK)]
+        cv = [cv_tiles[u][:, 0:H] for u in range(PACK)]
+        size = [size_tiles[u][:, 0:H] for u in range(PACK)]
         root = [tile([P, H], F32, f"root{u}") for u in range(PACK)]
         inv = [tile([P, H], F32, f"inv{u}") for u in range(PACK)]
-        den = [tile([P, H], F32, f"den{u}") for u in range(PACK)]
+        size_sum = [tile([P, H], F32, f"size_sum{u}") for u in range(PACK)]
         size4 = [tile([P, H], F32, f"size4_{u}") for u in range(PACK)]
-        cv3 = [tile([P, H], F32, "cv3_0")] + den[:-1]
+        cv3 = [tile([P, H], F32, "cv3_0")] + size_sum[:LAST]
+        cv_banks = b_banks
+        first_banks = [b_banks[0], a_banks[1]]
 
-        first_banks = [banks[0], banks[PACK + 1]]
-
-        def last_plane(u):
-            cols = slice(u * P, (u + 1) * P)
-            nc.vector.tensor_scalar(z_grouped[:, cols, early], ds[early][:, u::PACK], gt_t[:, early : early + 1], None, ALU.mult)
+        def round_last_tile(u):
+            nc.vector.tensor_scalar(z_grouped[:, u * P : (u + 1) * P, LAST], ds[LAST][:, u::PACK], gt_cols[:, LAST : LAST + 1], None, ALU.mult)
 
         def moments(u):
             cols = slice(u * P, (u + 1) * P)
             quantize(z_codes, z_scales, cols, z_grouped[:, cols, :].rearrange("p c t -> p (c t)"))
             if u == 0:
                 for h in range(2):
-                    product(first_banks[h], z_codes, z_scales, u, z2_codes, z2_scales, halves[h])
+                    product(first_banks[h], z_codes, z_scales, u, z2_codes, z2_scales, HALVES[h])
             else:
-                product(banks[u], z_codes, z_scales, u, z2_codes, z2_scales)
+                product(cv_banks[u], z_codes, z_scales, u, z2_codes, z2_scales)
 
-        def copy_values(u):
-            nc.vector.tensor_scalar(cv[u][:], banks[u][:], 0.0625, None, ALU.mult)
+        def copy_cv(u):
+            nc.vector.tensor_scalar(cv[u], cv_banks[u][:], CV_SCALE, None, ALU.mult)
 
-        def take_sizes(u):
-            nc.vector.scalar_tensor_tensor(size[u][:], banks[u][:], -0.0625, cv[u][:], ALU.mult, ALU.max)
+        def take_size(bank, u, cols=ALL):
+            nc.vector.scalar_tensor_tensor(size[u][:, cols], bank[:, cols], -CV_SCALE, cv[u][:, cols], ALU.mult, ALU.max)
 
-        def fetch(dst, src, lst, pieces=(slice(0, H),)):
+        def fetch(dst, src, offsets, pieces=(ALL,)):
             for cols in pieces:
-                nc.scalar.activation(dst[:, cols], src[:].indirect(lst[:, cols.start // 16 : cols.stop // 16]), ACT.Copy)
+                nc.scalar.activation(dst[:, cols], src[:].indirect(offsets[:, cols.start // LIST_ROWS : cols.stop // LIST_ROWS]), ACT.Copy)
 
         def inverse_root(u):
-            nc.vector.tensor_tensor(den[u][:], size4[u][:], size[u][:], ALU.add)
-            nc.scalar.activation(root[u][:], den[u][:], ACT.Abs_reciprocal_sqrt, bias=0.5)
+            nc.vector.tensor_tensor(size_sum[u][:], size4[u][:], size[u], ALU.add)
+            nc.scalar.activation(root[u][:], size_sum[u][:], ACT.Abs_reciprocal_sqrt, bias=0.5)
 
         def square(u):
             nc.vector.tensor_tensor(inv[u][:], root[u][:], root[u][:], ALU.mult)
 
         def finish(u):
             res = tile([P, H], F32, f"res{u}")
-            for cols in last_pieces if u == PACK - 1 else [slice(0, H)]:
+            for cols in LAST_PIECES if u == LAST else [ALL]:
                 nc.vector.tensor_tensor(res[:, cols], cv3[u][:, cols], inv[u][:, cols], ALU.mult)
                 nc.sync.dma_start(out_rows[:, u, cols], res[:, cols])
 
-        for pair in range(2):
-            last_plane(2 * pair)
-            last_plane(2 * pair + 1)
+        for pair in range(PACK // 2):
+            round_last_tile(2 * pair)
+            round_last_tile(2 * pair + 1)
             moments(2 * pair)
             moments(2 * pair + 1)
-        nc.scalar.activation(cv[0][:, halves[0]], first_banks[0][:, halves[0]], ACT.Copy, scale=0.0625)
-        nc.vector.tensor_scalar(cv[0][:, halves[1]], first_banks[1][:, halves[1]], 0.0625, None, ALU.mult)
-        fetch(cv3[0], cv_wide[0], n3_l)
+
+        nc.scalar.activation(cv[0][:, HALVES[0]], first_banks[0][:, HALVES[0]], ACT.Copy, scale=CV_SCALE)
+        nc.vector.tensor_scalar(cv[0][:, HALVES[1]], first_banks[1][:, HALVES[1]], CV_SCALE, None, ALU.mult)
+        fetch(cv3[0], cv_tiles[0], n3_l)
         for h in range(2):
-            nc.vector.scalar_tensor_tensor(size[0][:, halves[h]], first_banks[h][:, halves[h]], -0.0625, cv[0][:, halves[h]], ALU.mult, ALU.max)
-        fetch(size4[0], size_wide[0], n4_l)
-        copy_values(1)
-        copy_values(2)
+            take_size(first_banks[h], 0, HALVES[h])
+        fetch(size4[0], size_tiles[0], n4_l)
+
+        copy_cv(1)
+        copy_cv(2)
         for u in (1, 2):
-            take_sizes(u)
-            fetch(size4[u], size_wide[u], n4_l)
-        copy_values(3)
+            take_size(cv_banks[u], u)
+            fetch(size4[u], size_tiles[u], n4_l)
+        copy_cv(LAST)
         inverse_root(0)
-        take_sizes(3)
-        fetch(size4[3], size_wide[3], n4_l)
-        inverse_root(1)
-        fetch(cv3[1], cv_wide[1], n3_l)
-        inverse_root(2)
-        fetch(cv3[2], cv_wide[2], n3_l)
+        take_size(cv_banks[LAST], LAST)
+        fetch(size4[LAST], size_tiles[LAST], n4_l)
+
+        for u in (1, 2):
+            inverse_root(u)
+            fetch(cv3[u], cv_tiles[u], n3_l)
         square(0)
-        inverse_root(3)
-        fetch(cv3[3], cv_wide[3], n3_l, last_pieces)
+        inverse_root(LAST)
+        fetch(cv3[LAST], cv_tiles[LAST], n3_l, LAST_PIECES)
         finish(0)
         for u in range(1, PACK):
             square(u)

from contextlib import ExitStack

import concourse.mybir as mybir
from concourse.masks import make_identity

F32 = mybir.dt.float32
BF16 = mybir.dt.bfloat16
I32 = mybir.dt.int32
U32 = mybir.dt.uint32
U16 = mybir.dt.uint16
U8 = mybir.dt.uint8
FP8X4 = mybir.dt.float8_e4m3fn_x4
ALU = mybir.AluOpType
ACT = mybir.ActivationFunctionType

K, T, S, H, W = 512, 2048, 512, 512, 256
P = 128
PACK = 4
LAST = PACK - 1
RUN = 8
LINE = 4
LIST_ROWS = 16
HALF = H // 2
HALVES = [slice(0, HALF), slice(HALF, H)]
ALL = slice(0, H)
LAST_PIECES = [slice(0, HALF), slice(HALF, HALF + P), slice(HALF + P, H)]
CV_SCALE = 0.0625
FLOPS = 2 * (2 * K * S * H + S * H * H)


def tile_picked_momtputbnorm2_none_p_kernel(tc, x_words, x_scales, wa, wb, gt, gi, offs, two, n1, n2, n3, n4, out):
    nc = tc.nc
    with ExitStack() as ctx:
        lists = ctx.enter_context(tc.tile_pool(name="lists", bufs=1))
        sb = ctx.enter_context(tc.tile_pool(name="sb", bufs=1))
        psum = ctx.enter_context(tc.psum_pool(name="psum", bufs=1))

        def load_list(src, name):
            offsets = lists.tile(list(src.shape), U16, name=name)
            nc.sync.dma_start(offsets[:], src)
            return offsets

        def tile(shape, dtype, name):
            return sb.tile(shape, dtype, name=name, align_bytes=64)

        banks = [psum.tile([P, H], F32, name=f"bank{i}") for i in range(2 * PACK)]
        b_banks, a_banks = banks[:PACK], banks[PACK:]

        table_scales = tile([P, T], U8, "table_scales")
        nc.gpsimd.memset(table_scales[:].bitcast(I32), 0)
        for quad in range(4):
            queue = nc.sync if quad < 2 else nc.scalar
            queue.dma_start(table_scales[32 * quad : 32 * quad + 4, :].bitcast(I32), x_scales[0, 4 * quad : 4 * quad + 4, :].bitcast(I32))

        warm_in, warm_out = tile([P, 1], F32, "warm_in"), tile([P, 1], F32, "warm_out")
        nc.gpsimd.memset(warm_in[:], 1.0)
        nc.scalar.activation(warm_out[:], warm_in[:], ACT.Abs_reciprocal_sqrt, bias=0.5)

        two_l = load_list(two, "two_l")
        offs_l = load_list(offs, "offs_l")
        table_words = tile([P, T], U32, "table_words")
        nc.sync.dma_start(table_words[:].bitcast(I32), x_words[0].rearrange("p n j -> p (n j)").bitcast(I32))

        def load_weights(w, name):
            raws = [tile([P, PACK, HALF], F32, f"{name}{h}") for h in range(2)]
            for h in range(2):
                nc.sync.dma_start(raws[h][:], w.rearrange("(p j) c -> p j c", j=PACK)[:, :, HALVES[h]])
            return raws

        wb_raw = load_weights(wb, "wb_raw")
        wa_raw = load_weights(wa, "wa_raw")
        n2_l = load_list(n2, "n2_l")
        n1_l = load_list(n1, "n1_l")
        n4_l = load_list(n4, "n4_l")
        n3_l = load_list(n3, "n3_l")

        gain_rows = tile([P, P], F32, "gain_rows")
        nc.gpsimd.memset(gain_rows[:], 0.0)
        for first, src in ((0, gt), (PACK, gi)):
            nc.gpsimd.dma_start(
                gain_rows[first : first + PACK, :].rearrange("t (q r) -> t q r", r=RUN),
                src.rearrange("(q t r) o -> t q (r o)", t=PACK, r=RUN),
            )
        identity = tile([P, P], F32, "identity")
        make_identity(nc, identity[:])

        def pick_scales(offsets, name):
            picked = tile([P, S], U8, name + "_picked")
            nc.vector.tensor_copy(picked[:], table_scales[:].indirect(offsets[:]))
            dealt = tile([P, S], U8, name + "_dealt")
            nc.vector.tensor_copy(
                dealt[:].bitcast(I32).rearrange("p (t q w) -> p t q w", t=PACK, w=RUN // 4),
                picked[:].bitcast(I32).rearrange("p (q t w) -> p t q w", t=PACK, w=RUN // 4),
            )
            return dealt

        def pick_words(offsets, name):
            picked = tile([P, S], U32, name)
            nc.vector.tensor_copy(picked[:].rearrange("p (t q r) -> p q t r", t=PACK, r=RUN), table_words[:].indirect(offsets[:]))
            return picked

        def round_weights(raw, name):
            grouped = tile([P, HALF * PACK], BF16, name)
            nc.scalar.copy(
                grouped[:].rearrange("p (c i j) -> p c j i", i=LINE, j=PACK),
                raw[:].rearrange("p j (c i) -> p c j i", i=LINE),
            )
            return grouped

        def quantize(codes, scales, cols, values):
            nc.vector.quantize_mx(out=codes[:, cols].bitcast(FP8X4), scales=scales[:, cols], in_=values)

        def product(bank, l_codes, l_scales, block, r_codes, r_scales, r_cols=ALL):
            l_cols = slice(block * P, (block + 1) * P)
            nc.tensor.matmul_mx(
                out=bank[:, r_cols], lhsT=l_codes[:, l_cols].bitcast(FP8X4), lhsT_scale=l_scales[:, l_cols],
                rhs=r_codes[:, r_cols].bitcast(FP8X4), rhs_scale=r_scales[:, r_cols], start=True, stop=True,
            )

        two_scales = pick_scales(two_l, "two_scales")
        offs_scales = pick_scales(offs_l, "offs_scales")
        two_words = pick_words(two_l, "two_words")
        offs_words = pick_words(offs_l, "offs_words")

        wb_codes, wb_scales = tile([P, H], U32, "wb_codes"), tile([P, H], U8, "wb_scales")
        wa_codes, wa_scales = tile([P, H], U32, "wa_codes"), tile([P, H], U8, "wa_scales")
        for h in range(2):
            quantize(wb_codes, wb_scales, HALVES[h], round_weights(wb_raw[h], f"wb_grouped{h}")[:])
        for t in range(PACK):
            product(b_banks[t], two_words, two_scales, t, wb_codes, wb_scales)
        for h in range(2):
            quantize(wa_codes, wa_scales, HALVES[h], round_weights(wa_raw[h], f"wa_grouped{h}")[:])
        for t in range(PACK):
            product(a_banks[t], offs_words, offs_scales, t, wa_codes, wa_scales)

        cv_tiles = [tile([P, 2 * H if u < LAST else H], F32, f"cv_tile{u}") for u in range(PACK)]
        size_tiles = [tile([P, 2 * H], F32, f"size_tile{u}") for u in range(PACK)]
        b_rows = [cv_tiles[t][:, H:] for t in range(LAST)] + [tile([P, H], F32, "b_last")[:]]
        b_picked = [size_tiles[t][:, H : H + W] for t in range(PACK)]
        a_picked = [size_tiles[t][:, H + W :] for t in range(PACK)]
        for t in range(PACK):
            nc.vector.tensor_copy(b_rows[t], b_banks[t][:])
            nc.scalar.activation(b_picked[t], b_rows[t].indirect(n2_l[:]), ACT.Copy)

        ds = [tile([P, H], F32, f"ds{t}") for t in range(PACK)]
        z2_planes = tile([P, PACK * H], BF16, "z2_planes")
        ra = [tile([P, W], F32, f"ra{t}") for t in range(PACK)]
        for t in range(PACK):
            nc.vector.tensor_copy(ds[t][:], a_banks[t][:])
            nc.scalar.activation(a_picked[t], ds[t][:].indirect(n1_l[:]), ACT.Copy)
        for t in range(PACK):
            nc.vector.scalar_tensor_tensor(ra[t][:], a_picked[t], -0.5, b_picked[t], ALU.mult, ALU.add)
            nc.scalar.activation(ds[t][:].indirect(n1_l[:]), ra[t][:], ACT.Copy)

        nc.tensor.transpose(a_banks[0][:, 0:P], gain_rows[:], identity[:])
        gains = tile([P, 2 * PACK], F32, "gains")
        nc.vector.tensor_copy(gains[:], a_banks[0][:, 0 : 2 * PACK])
        gt_cols, gi_cols = gains[:, 0:PACK], gains[:, PACK : 2 * PACK]

        for t in range(PACK):
            nc.vector.tensor_scalar(z2_planes[:, t * H : (t + 1) * H], b_rows[t], gi_cols[:, t : t + 1], None, ALU.mult)
        z2_grouped = tile([P, H * PACK], BF16, "z2_grouped")
        nc.vector.tensor_copy(
            z2_grouped[:].rearrange("p (c i t) -> p c t i", i=LINE, t=PACK),
            z2_planes[:].rearrange("p (t c i) -> p c t i", i=LINE, t=PACK),
        )
        z2_codes, z2_scales = tile([P, H], U32, "z2_codes"), tile([P, H], U8, "z2_scales")
        quantize(z2_codes, z2_scales, ALL, z2_grouped[:])

        z_grouped = tile([P, H, PACK], BF16, "z_grouped")
        for t in range(LAST):
            nc.vector.tensor_scalar(
                z_grouped[:, :, t].rearrange("p (u m) -> p m u", u=PACK),
                ds[t][:].rearrange("p (m u) -> p m u", u=PACK),
                gt_cols[:, t : t + 1], None, ALU.mult,
            )
        z_codes, z_scales = tile([P, H], U32, "z_codes"), tile([P, H], U8, "z_scales")

        out_rows = out.rearrange("(p u) c -> p u c", u=PACK)
        cv = [cv_tiles[u][:, 0:H] for u in range(PACK)]
        size = [size_tiles[u][:, 0:H] for u in range(PACK)]
        root = [tile([P, H], F32, f"root{u}") for u in range(PACK)]
        inv = [tile([P, H], F32, f"inv{u}") for u in range(PACK)]
        size_sum = [tile([P, H], F32, f"size_sum{u}") for u in range(PACK)]
        size4 = [tile([P, H], F32, f"size4_{u}") for u in range(PACK)]
        cv3 = [tile([P, H], F32, "cv3_0")] + size_sum[:LAST]
        cv_banks = b_banks
        first_banks = [b_banks[0], a_banks[1]]

        def round_last_tile(u):
            nc.vector.tensor_scalar(z_grouped[:, u * P : (u + 1) * P, LAST], ds[LAST][:, u::PACK], gt_cols[:, LAST : LAST + 1], None, ALU.mult)

        def moments(u):
            cols = slice(u * P, (u + 1) * P)
            quantize(z_codes, z_scales, cols, z_grouped[:, cols, :].rearrange("p c t -> p (c t)"))
            if u == 0:
                for h in range(2):
                    product(first_banks[h], z_codes, z_scales, u, z2_codes, z2_scales, HALVES[h])
            else:
                product(cv_banks[u], z_codes, z_scales, u, z2_codes, z2_scales)

        def copy_cv(u):
            nc.vector.tensor_scalar(cv[u], cv_banks[u][:], CV_SCALE, None, ALU.mult)

        def take_size(bank, u, cols=ALL):
            nc.vector.scalar_tensor_tensor(size[u][:, cols], bank[:, cols], -CV_SCALE, cv[u][:, cols], ALU.mult, ALU.max)

        def fetch(dst, src, offsets, pieces=(ALL,)):
            for cols in pieces:
                nc.scalar.activation(dst[:, cols], src[:].indirect(offsets[:, cols.start // LIST_ROWS : cols.stop // LIST_ROWS]), ACT.Copy)

        def inverse_root(u):
            nc.vector.tensor_tensor(size_sum[u][:], size4[u][:], size[u], ALU.add)
            nc.scalar.activation(root[u][:], size_sum[u][:], ACT.Abs_reciprocal_sqrt, bias=0.5)

        def square(u):
            nc.vector.tensor_tensor(inv[u][:], root[u][:], root[u][:], ALU.mult)

        def finish(u):
            res = tile([P, H], F32, f"res{u}")
            for cols in LAST_PIECES if u == LAST else [ALL]:
                nc.vector.tensor_tensor(res[:, cols], cv3[u][:, cols], inv[u][:, cols], ALU.mult)
                nc.sync.dma_start(out_rows[:, u, cols], res[:, cols])

        for pair in range(PACK // 2):
            round_last_tile(2 * pair)
            round_last_tile(2 * pair + 1)
            moments(2 * pair)
            moments(2 * pair + 1)

        nc.scalar.activation(cv[0][:, HALVES[0]], first_banks[0][:, HALVES[0]], ACT.Copy, scale=CV_SCALE)
        nc.vector.tensor_scalar(cv[0][:, HALVES[1]], first_banks[1][:, HALVES[1]], CV_SCALE, None, ALU.mult)
        fetch(cv3[0], cv_tiles[0], n3_l)
        for h in range(2):
            take_size(first_banks[h], 0, HALVES[h])
        fetch(size4[0], size_tiles[0], n4_l)

        copy_cv(1)
        copy_cv(2)
        for u in (1, 2):
            take_size(cv_banks[u], u)
            fetch(size4[u], size_tiles[u], n4_l)
        copy_cv(LAST)
        inverse_root(0)
        take_size(cv_banks[LAST], LAST)
        fetch(size4[LAST], size_tiles[LAST], n4_l)

        for u in (1, 2):
            inverse_root(u)
            fetch(cv3[u], cv_tiles[u], n3_l)
        square(0)
        inverse_root(LAST)
        fetch(cv3[LAST], cv_tiles[LAST], n3_l, LAST_PIECES)
        finish(0)
        for u in range(1, PACK):
            square(u)
            finish(u)
